import numpy as np
import ml_dtypes


def mxq(x, axis, fmt="e4m3"):
    dtype, down = {"e4m3": (ml_dtypes.float8_e4m3fn, 7), "e5m2": (ml_dtypes.float8_e5m2, 14)}[fmt]
    v = np.moveaxis(np.asarray(x, np.float32).astype(ml_dtypes.bfloat16).astype(np.float64), axis, -1)
    blocks = v.reshape(v.shape[:-1] + (-1, 32))
    amax = np.abs(blocks).max(-1, keepdims=True)
    byte = np.maximum(np.where(amax > 0, np.frexp(amax)[1] - 1 + 127, 0) - down, 1)
    scale = np.exp2(byte - 127.0)
    codes = (blocks / scale).astype(np.float32).astype(dtype).astype(np.float64)
    return np.moveaxis((codes * scale).reshape(v.shape), -1, axis)


WIDE = False


def mx_kscale(k):
    if not WIDE:
        return np.ones(k)
    levels = np.array([10, -10, 5, -5, 0])
    if k % 512:
        return np.exp2(np.random.permutation(np.resize(levels, k // 32))).repeat(32)
    a = np.empty((k // 512, 16))
    for p in range(k // 512):
        a[p, :8] = np.random.permutation(np.resize(levels, 8))
        for g in range(8):
            far = levels[np.abs(levels - a[p, g]) >= 10]
            a[p, g + 8] = far[np.random.randint(len(far))]
    return np.exp2(a.ravel()).repeat(32)


def f64(x):
    return np.asarray(x).astype(np.float64)


def striped(idx):
    return np.tile(idx.reshape(-1, 16).T, (8, 1)).astype(np.uint16)


def unstriped(offs):
    return offs[:16].T.reshape(-1).astype(np.int64)


E2M1 = np.array([0.0, 0.5, 1.0, 1.5, 2.0, 3.0, 4.0, 6.0, -0.0, -0.5, -1.0, -1.5, -2.0, -3.0, -4.0, -6.0])


def pack_weight(w, fmt):
    k, n = w.shape
    w = f64(np.asarray(w, np.float32).astype(ml_dtypes.bfloat16)).reshape(k // 32, 32, n)
    amax = np.abs(w).max(1)
    if fmt == "e4m3":
        byte = np.frexp(amax)[1] - 1 + 127 - 7
    else:
        mant, ex = np.frexp(amax / 6.0)
        byte = np.where(mant > 0.5, ex, ex - 1) + 127
    byte = np.clip(np.where(amax > 0, byte, 1), 1, 254)
    scaled = (w * np.exp2(127.0 - byte)[:, None, :]).reshape(k, n).astype(np.float32)
    by_word = np.ascontiguousarray(scaled.reshape(k // 512, 128, 4, n).transpose(0, 1, 3, 2))
    if fmt == "e4m3":
        words = by_word.astype(ml_dtypes.float8_e4m3fn).view(np.uint8)
    else:
        c = by_word.astype(ml_dtypes.float4_e2m1fn).view(np.uint8) & 0xF
        words = (c[..., 0::2] | (c[..., 1::2] << 4)).reshape(k // 512, 128, 2 * n)
    return np.ascontiguousarray(words), np.ascontiguousarray(byte.astype(np.uint8).reshape(k // 512, 16, n))


def unpack_weight(words, scales, fmt):
    g, _, n = scales.shape
    words = np.ascontiguousarray(words).reshape(g, 128, n, -1)
    if fmt == "e4m3":
        vals = words.view(ml_dtypes.float8_e4m3fn).astype(np.float64)
    else:
        nib = np.empty((g, 128, n, 4), np.uint8)
        nib[..., 0::2] = words & 0xF
        nib[..., 1::2] = words >> 4
        vals = E2M1[nib]
    vals = vals * np.repeat(np.exp2(scales.astype(np.float64) - 127.0), 8, axis=1)[..., None]
    return vals.transpose(0, 1, 3, 2).reshape(g * 512, n)


K, T, E, C, N = 2560, 1280, 15, 256, 128
TOP = 3


def by_expert(wq, xq):
    return np.concatenate([wq[e].T @ xq[:, e * C:(e + 1) * C] for e in range(E)], axis=1)


def setup_inputs():
    n = np.random.standard_normal
    s = mx_kscale(K)[:, None]
    deal = np.repeat(np.arange(E), C).reshape(TOP, T)[:, np.random.permutation(T)]
    deal = np.take_along_axis(deal, np.argsort(np.random.rand(TOP, T), axis=0), axis=0)
    for _ in range(8):
        s_, t_ = np.random.permutation(T).reshape(2, -1); r = np.random.randint(TOP, size=T // 2); x, y = deal[r, s_].copy(), deal[r, t_].copy()
        ok = ~((deal[:, s_] == y).any(0) | (deal[:, t_] == x).any(0)); deal[r[ok], s_[ok]] = y[ok]; deal[r[ok], t_[ok]] = x[ok]
    order = np.lexsort((np.random.rand(TOP * T), deal.reshape(-1)))
    slot_token = order % T; pos = np.empty(TOP * T, np.int64); pos[order] = np.arange(TOP * T); pos = pos.reshape(TOP, T)
    g = np.random.uniform(0.5, 1.5, (TOP, T)); g = g / g.sum(0)
    x = pack_weight(n((K, T)) * s, "e4m3")
    return {
        "x_words": x[0],
        "x_scales": x[1],
        "w": (n((E, K, N)) / np.sqrt(K) / s[None]).astype(np.float32),
        "gate": np.stack([np.tile(r, (N, 1)) for r in g]).astype(np.float32),
        "offs": striped(slot_token),
        "pos1": striped(pos[0]),
        "pos2": striped(pos[1]),
        "pos3": striped(pos[2]),
    }


def reference(x_words, x_scales, w, gate, offs, pos1, pos2, pos3):
    idx = unstriped(offs)
    xq = unpack_weight(x_words, x_scales, "e4m3")[:, idx]
    y = by_expert(mxq(f64(w), 1, "e4m3"), xq)
    return sum(f64(gate[r]) * y[:, unstriped(p)] for r, p in enumerate((pos1, pos2, pos3)))

@@ -1,0 +1,193 @@
+from contextlib import ExitStack
+
+import concourse.mybir as mybir
+
+K, T, E, C, N = 2560, 1280, 15, 256, 128
+TOP = 3
+SLOTS = E * C
+FLOPS = 2 * K * N * SLOTS
+
+F32 = mybir.dt.float32
+BF16 = mybir.dt.bfloat16
+I32 = mybir.dt.int32
+U32 = mybir.dt.uint32
+U16 = mybir.dt.uint16
+U8 = mybir.dt.uint8
+FP8X4 = mybir.dt.float8_e4m3fn_x4
+MULT = mybir.AluOpType.mult
+ADD = mybir.AluOpType.add
+
+P = 128
+PACK = 4
+PASSES = K // (P * PACK)
+GROUP = 5
+GROUP_SLOTS = GROUP * C
+WORD_SPARE = 512
+SCALE_PIECE = SLOTS // 2
+RAW_BUFS = 5
+CODE_BUFS = 7
+SUM_BANKS = 7
+Y_AFTER = 6
+CHUNKS = (640, 384, 256)
+
+
+def tile_moe_pkd_lin_none_kernel(tc, x_words, x_scales, w, gate, offs, pos1, pos2, pos3, out):
+    nc = tc.nc
+    with ExitStack() as ctx:
+        held = ctx.enter_context(tc.tile_pool(name="held", bufs=1))
+        ring = ctx.enter_context(tc.tile_pool(name="ring", bufs=1))
+        psum = ctx.enter_context(tc.psum_pool(name="psum", bufs=1))
+
+        offs_sb = held.tile([P, SLOTS // 16], U16, name="offs_sb")
+        pos_sb = [held.tile([P, T // 16], U16, name="pos_sb%d" % r) for r in range(TOP)]
+        words = held.tile([P, PASSES * T + WORD_SPARE], I32, name="words", align_bytes=64)
+        scales = held.tile([P, SLOTS], U8, name="scales", align_bytes=64)
+        slot_scales = held.tile([P, SLOTS], U8, name="slot_scales", align_bytes=64)
+        last_scales = held.tile([P, SLOTS], U8, name="last_scales", align_bytes=64)
+        gate_sb = [held.tile([P, T], F32, name="gate_sb%d" % r) for r in range(TOP)]
+
+        def word_start(o):
+            return (PASSES - 1 - o) * T
+
+        def load_words(o):
+            nc.sync.dma_start(
+                out=words[:, word_start(o) : word_start(o) + T],
+                in_=x_words[o].rearrange("p t r -> p (t r)").bitcast(I32),
+            )
+
+        raw = {}
+
+        def load_weights(e):
+            if e == Y_AFTER:
+                raw[e] = held.tile([P, PASSES, PACK, N], F32, name="raw_y", tag="y")
+            else:
+                raw[e] = ring.tile([P, PASSES, PACK, N], F32, name="raw", tag="raw", bufs=RAW_BUFS)
+            nc.sync.dma_start(out=raw[e][:], in_=w[e].rearrange("(o p j) n -> p o j n", p=P, j=PACK))
+
+        nc.vector.memset(words[:, PASSES * T :], 0)
+        scales32 = scales[:].bitcast(I32)
+        nc.vector.memset(scales32[:, : T // 4], 0)
+        nc.vector.memset(scales32[:, T // 4 :], 0)
+        nc.vector.memset(last_scales[:].bitcast(I32), 0)
+
+        nc.sync.dma_start(offs_sb[:], offs)
+        load_words(0)
+        xs32 = x_scales.bitcast(I32)
+        for q in range(4):
+            nc.sync.dma_start(out=scales32[32 * q : 32 * q + 16, : T // 4], in_=xs32[0:4, 4 * q : 4 * q + 4, :])
+        nc.sync.dma_start(out=scales32[16:32, : T // 4], in_=xs32[4])
+
+        gathered = {}
+
+        def gather_words(i):
+            g, o = divmod(i, PASSES)
+            gathered[i] = held.tile([P, GROUP_SLOTS], U32, name="gathered", tag="slot%d" % i, align_bytes=64)
+            window = words[:, word_start(o) : word_start(o) + T + WORD_SPARE].bitcast(U32)
+            cols = GROUP_SLOTS // 16
+            nc.vector.tensor_copy(gathered[i][:], window.indirect(offs_sb[:, g * cols : (g + 1) * cols]))
+
+        gather_words(0)
+        for h in range(SLOTS // SCALE_PIECE):
+            cols = SCALE_PIECE // 16
+            nc.vector.tensor_copy(
+                slot_scales[:, h * SCALE_PIECE : (h + 1) * SCALE_PIECE],
+                scales[:].indirect(offs_sb[:, h * cols : (h + 1) * cols]),
+            )
+
+        rounded, codes, code_scales, sums = {}, {}, {}, {}
+
+        def cast(e):
+            rounded[e] = held.tile([P, PASSES, N, PACK], BF16, name="rounded", tag="slot%d" % (e + 1), align_bytes=64)
+            nc.scalar.copy(
+                out=rounded[e][:].rearrange("p o (c i) j -> p o c j i", i=4),
+                in_=raw[e][:].rearrange("p o j (c i) -> p o c j i", i=4),
+            )
+
+        def quantise(e):
+            codes[e] = ring.tile([P, PASSES * N], U32, name="codes", tag="codes", bufs=CODE_BUFS, align_bytes=64)
+            code_scales[e] = ring.tile([P, PASSES * N], U8, name="code_scales", tag="code_scales", bufs=CODE_BUFS, align_bytes=64)
+            flat = rounded[e][:].rearrange("p o n j -> p (o n j)")
+            for a, b in ((0, 4 * N), (4 * N, 5 * N)):
+                nc.vector.quantize_mx(
+                    out=codes[e][:, a:b].bitcast(FP8X4), scales=code_scales[e][:, a:b], in_=flat[:, PACK * a : PACK * b]
+                )
+
+        def multiply(e, o):
+            g, c = divmod(e, GROUP)
+            if o == 0:
+                sums[e] = psum.tile([P, C], F32, name="sums", tag="bank%d" % (e % SUM_BANKS))
+            if o < PASSES - 1:
+                plane = slot_scales[4 * o : P, e * C : (e + 1) * C]
+            else:
+                plane = last_scales[:, e * C : (e + 1) * C]
+            nc.tensor.matmul_mx(
+                out=sums[e][:],
+                lhsT=codes[e][:, o * N : (o + 1) * N].bitcast(FP8X4),
+                lhsT_scale=code_scales[e][:, o * N : (o + 1) * N],
+                rhs=gathered[g * PASSES + o][:, c * C : (c + 1) * C].bitcast(FP8X4),
+                rhs_scale=plane,
+                start=(o == 0),
+                stop=(o == PASSES - 1),
+            )
+
+        ys = []
+
+        def copy_out(e):
+            if not ys:
+                ys.append(held.tile([P, SLOTS], F32, name="y", tag="y"))
+            nc.scalar.copy(out=ys[0][:, e * C : (e + 1) * C], in_=sums[e][:])
+
+        load_weights(0)
+        for o in range(1, PASSES):
+            load_words(o)
+            load_weights(o)
+        for q in range(4):
+            nc.sync.dma_start(
+                out=last_scales[:].bitcast(I32)[32 * q : 32 * q + 4, :],
+                in_=slot_scales[:].bitcast(I32)[16 + 4 * q : 20 + 4 * q, :],
+            )
+        for r, pos in enumerate((pos1, pos2, pos3)):
+            nc.sync.dma_start(pos_sb[r][:], pos)
+
+        cast(0)
+        for e in range(E):
+            g, c = divmod(e, GROUP)
+            if e + RAW_BUFS < E:
+                load_weights(e + RAW_BUFS)
+            if e + RAW_BUFS == E:
+                for r in range(TOP):
+                    nc.sync.dma_start(out=gate_sb[r][:], in_=gate[r])
+            if e + 1 < E:
+                cast(e + 1)
+            if g > 0 and c == 0:
+                for d in range(e - GROUP, e - 1):
+                    copy_out(d)
+            if g > 0 and c == 1:
+                copy_out(e - 2)
+            quantise(e)
+            for o in range(c + 1):
+                multiply(e, o)
+            if c + 1 < GROUP:
+                gather_words(e + 1)
+                for d in range(e - c, e + 1):
+                    multiply(d, c + 1)
+            elif e + 1 < E:
+                gather_words(e + 1)
+        for d in range(E - GROUP, E):
+            copy_out(d)
+
+        y = ys[0]
+        prods = [held.tile([P, T], F32, name="prod%d" % r, tag="slot%d" % r, align_bytes=64) for r in range(TOP)]
+        part = held.tile([P, T], F32, name="part", tag="slot3", align_bytes=64)
+        total = held.tile([P, T], F32, name="total", tag="slot4", align_bytes=64)
+        t0 = 0
+        for width in CHUNKS:
+            cols = slice(t0, t0 + width)
+            for r in range(TOP):
+                nc.vector.tensor_tensor(
+                    prods[r][:, cols], y[:].indirect(pos_sb[r][:, t0 // 16 : (t0 + width) // 16]), gate_sb[r][:, cols], MULT
+                )
+            nc.vector.tensor_tensor(part[:, cols], prods[0][:, cols], prods[1][:, cols], ADD)
+            nc.vector.tensor_tensor(total[:, cols], part[:, cols], prods[2][:, cols], ADD)
+            nc.sync.dma_start(out=out[:, cols], in_=total[:, cols])
+            t0 = t0 + width

@@ -1,6 +1,7 @@
 from contextlib import ExitStack
 
 import concourse.mybir as mybir
+from concourse.masks import make_identity
 
 K, T, E, C, N = 2560, 1280, 15, 256, 128
 TOP = 3
@@ -22,13 +23,17 @@ PACK = 4
 PASSES = K // (P * PACK)
 GROUP = 5
 GROUP_SLOTS = GROUP * C
+GATHERS = PASSES * (E // GROUP)
 WORD_SPARE = 512
 SCALE_PIECE = SLOTS // 2
 RAW_BUFS = 5
-CODE_BUFS = 7
-SUM_BANKS = 7
-Y_AFTER = 6
-CHUNKS = (640, 384, 256)
+CODE_BUFS = 4
+BANKS = 8
+BANK = 512
+Y_AFTER = 7
+SETS = [(e, min(e + 2, E)) for e in range(0, E, 2)]
+LAST_PIECES = ((0, 2), (2, 4), (4, 5))
+TURNED = 2 * BANK
 
 
 def tile_moe_pkd_lin_none_kernel(tc, x_words, x_scales, w, gate, offs, pos1, pos2, pos3, out):
@@ -45,6 +50,7 @@ def tile_moe_pkd_lin_none_kernel(tc, x_words, x_scales, w, gate, offs, pos1, pos
         slot_scales = held.tile([P, SLOTS], U8, name="slot_scales", align_bytes=64)
         last_scales = held.tile([P, SLOTS], U8, name="last_scales", align_bytes=64)
         gate_sb = [held.tile([P, T], F32, name="gate_sb%d" % r) for r in range(TOP)]
+        ident = held.tile([P, P], F32, name="ident")
 
         def word_start(o):
             return (PASSES - 1 - o) * T
@@ -64,83 +70,28 @@ def tile_moe_pkd_lin_none_kernel(tc, x_words, x_scales, w, gate, offs, pos1, pos
                 raw[e] = ring.tile([P, PASSES, PACK, N], F32, name="raw", tag="raw", bufs=RAW_BUFS)
             nc.sync.dma_start(out=raw[e][:], in_=w[e].rearrange("(o p j) n -> p o j n", p=P, j=PACK))
 
-        nc.vector.memset(words[:, PASSES * T :], 0)
         scales32 = scales[:].bitcast(I32)
         nc.vector.memset(scales32[:, : T // 4], 0)
         nc.vector.memset(scales32[:, T // 4 :], 0)
+        nc.vector.memset(words[:, PASSES * T :], 0)
         nc.vector.memset(last_scales[:].bitcast(I32), 0)
+        make_identity(nc, ident[:])
 
         nc.sync.dma_start(offs_sb[:], offs)
-        load_words(0)
         xs32 = x_scales.bitcast(I32)
         for q in range(4):
             nc.sync.dma_start(out=scales32[32 * q : 32 * q + 16, : T // 4], in_=xs32[0:4, 4 * q : 4 * q + 4, :])
         nc.sync.dma_start(out=scales32[16:32, : T // 4], in_=xs32[4])
+        for o in range(PASSES):
+            load_weights(o)
+            load_words(o)
 
-        gathered = {}
-
-        def gather_words(i):
-            g, o = divmod(i, PASSES)
-            gathered[i] = held.tile([P, GROUP_SLOTS], U32, name="gathered", tag="slot%d" % i, align_bytes=64)
-            window = words[:, word_start(o) : word_start(o) + T + WORD_SPARE].bitcast(U32)
-            cols = GROUP_SLOTS // 16
-            nc.vector.tensor_copy(gathered[i][:], window.indirect(offs_sb[:, g * cols : (g + 1) * cols]))
-
-        gather_words(0)
         for h in range(SLOTS // SCALE_PIECE):
             cols = SCALE_PIECE // 16
             nc.vector.tensor_copy(
                 slot_scales[:, h * SCALE_PIECE : (h + 1) * SCALE_PIECE],
                 scales[:].indirect(offs_sb[:, h * cols : (h + 1) * cols]),
             )
-
-        rounded, codes, code_scales, sums = {}, {}, {}, {}
-
-        def cast(e):
-            rounded[e] = held.tile([P, PASSES, N, PACK], BF16, name="rounded", tag="slot%d" % (e + 1), align_bytes=64)
-            nc.scalar.copy(
-                out=rounded[e][:].rearrange("p o (c i) j -> p o c j i", i=4),
-                in_=raw[e][:].rearrange("p o j (c i) -> p o c j i", i=4),
-            )
-
-        def quantise(e):
-            codes[e] = ring.tile([P, PASSES * N], U32, name="codes", tag="codes", bufs=CODE_BUFS, align_bytes=64)
-            code_scales[e] = ring.tile([P, PASSES * N], U8, name="code_scales", tag="code_scales", bufs=CODE_BUFS, align_bytes=64)
-            flat = rounded[e][:].rearrange("p o n j -> p (o n j)")
-            for a, b in ((0, 4 * N), (4 * N, 5 * N)):
-                nc.vector.quantize_mx(
-                    out=codes[e][:, a:b].bitcast(FP8X4), scales=code_scales[e][:, a:b], in_=flat[:, PACK * a : PACK * b]
-                )
-
-        def multiply(e, o):
-            g, c = divmod(e, GROUP)
-            if o == 0:
-                sums[e] = psum.tile([P, C], F32, name="sums", tag="bank%d" % (e % SUM_BANKS))
-            if o < PASSES - 1:
-                plane = slot_scales[4 * o : P, e * C : (e + 1) * C]
-            else:
-                plane = last_scales[:, e * C : (e + 1) * C]
-            nc.tensor.matmul_mx(
-                out=sums[e][:],
-                lhsT=codes[e][:, o * N : (o + 1) * N].bitcast(FP8X4),
-                lhsT_scale=code_scales[e][:, o * N : (o + 1) * N],
-                rhs=gathered[g * PASSES + o][:, c * C : (c + 1) * C].bitcast(FP8X4),
-                rhs_scale=plane,
-                start=(o == 0),
-                stop=(o == PASSES - 1),
-            )
-
-        ys = []
-
-        def copy_out(e):
-            if not ys:
-                ys.append(held.tile([P, SLOTS], F32, name="y", tag="y"))
-            nc.scalar.copy(out=ys[0][:, e * C : (e + 1) * C], in_=sums[e][:])
-
-        load_weights(0)
-        for o in range(1, PASSES):
-            load_words(o)
-            load_weights(o)
         for q in range(4):
             nc.sync.dma_start(
                 out=last_scales[:].bitcast(I32)[32 * q : 32 * q + 4, :],
@@ -149,45 +100,137 @@ def tile_moe_pkd_lin_none_kernel(tc, x_words, x_scales, w, gate, offs, pos1, pos
         for r, pos in enumerate((pos1, pos2, pos3)):
             nc.sync.dma_start(pos_sb[r][:], pos)
 
+        rounded, codes, code_scales, sums, gathered = {}, {}, {}, {}, {}
+        passes_gathered = [0] * E
+        passes_done = [0] * E
+        ys = []
+
+        def cast(s):
+            a, b = SETS[s]
+            rounded[s] = held.tile([P, (b - a) * K], BF16, name="rounded", tag="slot%d" % s, align_bytes=64)
+            for e in range(a, b):
+                nc.scalar.copy(
+                    out=rounded[s][:, (e - a) * K : (e - a + 1) * K].rearrange("p (o c i j) -> p o c j i", o=PASSES, i=4, j=PACK),
+                    in_=raw[e][:].rearrange("p o j (c i) -> p o c j i", i=4),
+                )
+                if e + RAW_BUFS < E:
+                    load_weights(e + RAW_BUFS)
+
+        def multiply():
+            for e in sorted(codes):
+                g, c = divmod(e, GROUP)
+                for o in range(passes_done[e], passes_gathered[e]):
+                    if o == 0:
+                        sums[e] = psum.tile([P, C], F32, name="sums", tag="bank%d" % (e % BANKS))
+                    if o < PASSES - 1:
+                        plane = slot_scales[4 * o : P, e * C : (e + 1) * C]
+                    else:
+                        plane = last_scales[:, e * C : (e + 1) * C]
+                    nc.tensor.matmul_mx(
+                        out=sums[e][:],
+                        lhsT=codes[e][:, o * N : (o + 1) * N].bitcast(FP8X4),
+                        lhsT_scale=code_scales[e][:, o * N : (o + 1) * N],
+                        rhs=gathered[g * PASSES + o][:, c * C : (c + 1) * C].bitcast(FP8X4),
+                        rhs_scale=plane,
+                        start=(o == 0),
+                        stop=(o == PASSES - 1),
+                    )
+                passes_done[e] = passes_gathered[e]
+
+        def quantise(s):
+            a, b = SETS[s]
+            width = (b - a) * PASSES * N
+            set_codes = ring.tile([P, width], U32, name="set_codes", tag="codes", bufs=CODE_BUFS, align_bytes=64)
+            set_scales = ring.tile([P, width], U8, name="set_scales", tag="code_scales", bufs=CODE_BUFS, align_bytes=64)
+            cut = width * 4 // 5
+            for lo, hi in ((0, cut), (cut, width)):
+                nc.vector.quantize_mx(
+                    out=set_codes[:, lo:hi].bitcast(FP8X4), scales=set_scales[:, lo:hi], in_=rounded[s][:, PACK * lo : PACK * hi]
+                )
+            for e in range(a, b):
+                codes[e] = set_codes[:, (e - a) * PASSES * N : (e - a + 1) * PASSES * N]
+                code_scales[e] = set_scales[:, (e - a) * PASSES * N : (e - a + 1) * PASSES * N]
+            multiply()
+
+        def gather_words(first, count, tag):
+            dest = held.tile([P, count * GROUP_SLOTS], U32, name="dest", tag=tag, align_bytes=64)
+            for i in range(first, first + count):
+                g, o = divmod(i, PASSES)
+                gathered[i] = dest[:, (i - first) * GROUP_SLOTS : (i - first + 1) * GROUP_SLOTS]
+                window = words[:, word_start(o) : word_start(o) + T + WORD_SPARE].bitcast(U32)
+                for a, b in LAST_PIECES if i == GATHERS - 1 else ((0, GROUP),):
+                    cols = slice((g * GROUP + a) * C // 16, (g * GROUP + b) * C // 16)
+                    nc.vector.tensor_copy(gathered[i][:, a * C : b * C], window.indirect(offs_sb[:, cols]))
+                    for e in range(g * GROUP + a, g * GROUP + b):
+                        passes_gathered[e] = o + 1
+                    multiply()
+
+        def copy_out(experts):
+            if not ys:
+                ys.append(held.tile([P, SLOTS], F32, name="y", tag="y"))
+            for e in experts:
+                nc.scalar.copy(out=ys[0][:, e * C : (e + 1) * C], in_=sums[e][:])
+
+        gather_words(0, 2, "lead")
         cast(0)
-        for e in range(E):
-            g, c = divmod(e, GROUP)
-            if e + RAW_BUFS < E:
-                load_weights(e + RAW_BUFS)
-            if e + RAW_BUFS == E:
+        for s in range(len(SETS)):
+            if s + 1 < len(SETS):
+                cast(s + 1)
+            if s == 4:
                 for r in range(TOP):
                     nc.sync.dma_start(out=gate_sb[r][:], in_=gate[r])
-            if e + 1 < E:
-                cast(e + 1)
-            if g > 0 and c == 0:
-                for d in range(e - GROUP, e - 1):
-                    copy_out(d)
-            if g > 0 and c == 1:
-                copy_out(e - 2)
-            quantise(e)
-            for o in range(c + 1):
-                multiply(e, o)
-            if c + 1 < GROUP:
-                gather_words(e + 1)
-                for d in range(e - c, e + 1):
-                    multiply(d, c + 1)
-            elif e + 1 < E:
-                gather_words(e + 1)
-        for d in range(E - GROUP, E):
-            copy_out(d)
+            if s == 3:
+                copy_out(range(0, GROUP))
+            if s == 5:
+                copy_out(range(GROUP, 2 * GROUP))
+            quantise(s)
+            if s < 6:
+                gather_words(2 * s + 2, 2, "slot%d" % s)
+            if s == 7:
+                gather_words(GATHERS - 1, 1, "slot%d" % s)
+        copy_out(range(2 * GROUP, E))
 
         y = ys[0]
         prods = [held.tile([P, T], F32, name="prod%d" % r, tag="slot%d" % r, align_bytes=64) for r in range(TOP)]
-        part = held.tile([P, T], F32, name="part", tag="slot3", align_bytes=64)
+        turned_sb = held.tile([P, TURNED], F32, name="turned_sb", tag="slot3", align_bytes=64)
         total = held.tile([P, T], F32, name="total", tag="slot4", align_bytes=64)
-        t0 = 0
-        for width in CHUNKS:
-            cols = slice(t0, t0 + width)
-            for r in range(TOP):
-                nc.vector.tensor_tensor(
-                    prods[r][:, cols], y[:].indirect(pos_sb[r][:, t0 // 16 : (t0 + width) // 16]), gate_sb[r][:, cols], MULT
+        part = held.tile([P, T - TURNED], F32, name="part", tag="slot5", align_bytes=64)
+        turned = [psum.tile([P, BANK], F32, name="turned%d" % u, tag="bank%d" % u) for u in range(2)]
+
+        def product(r, a, b):
+            nc.vector.tensor_tensor(prods[r][:, a:b], y[:].indirect(pos_sb[r][:, a // 16 : b // 16]), gate_sb[r][:, a:b], MULT)
+
+        def add_turned(r, u):
+            for k in range(BANK // P):
+                nc.tensor.matmul(
+                    turned[u][:, k * P : (k + 1) * P],
+                    prods[r][:, u * BANK + k * P : u * BANK + (k + 1) * P],
+                    ident[:],
+                    is_transpose=True,
+                    start=(r == 0 and k == 0),
+                    stop=(r == TOP - 1 and k == BANK // P - 1),
                 )
-            nc.vector.tensor_tensor(part[:, cols], prods[0][:, cols], prods[1][:, cols], ADD)
-            nc.vector.tensor_tensor(total[:, cols], part[:, cols], prods[2][:, cols], ADD)
+
+        def turn_back(u):
+            cols = slice(u * BANK, (u + 1) * BANK)
+            nc.scalar.copy(out=turned_sb[:, cols], in_=turned[u][:])
+            back = psum.tile([P, BANK], F32, name="back", tag="bank%d" % (2 + u))
+            for k in range(BANK // P):
+                nc.tensor.transpose(back[:, k * P : (k + 1) * P], turned_sb[:, u * BANK + k * P : u * BANK + (k + 1) * P], ident[:])
+            nc.scalar.copy(out=total[:, cols], in_=back[:])
             nc.sync.dma_start(out=out[:, cols], in_=total[:, cols])
-            t0 = t0 + width
+
+        for r in range(TOP - 1):
+            product(r, 0, TURNED)
+            for u in range(2):
+                add_turned(r, u)
+        for u in range(2):
+            product(TOP - 1, u * BANK, (u + 1) * BANK)
+            add_turned(TOP - 1, u)
+            turn_back(u)
+        product(0, TURNED, T)
+        product(1, TURNED, T)
+        product(2, TURNED, T)
+        nc.vector.tensor_tensor(part[:], prods[0][:, TURNED:], prods[1][:, TURNED:], ADD)
+        nc.vector.tensor_tensor(total[:, TURNED:], part[:], prods[2][:, TURNED:], ADD)
+        nc.sync.dma_start(out=out[:, TURNED:], in_=total[:, TURNED:])

@@ -26,11 +26,12 @@ GROUP_SLOTS = GROUP * C
 GATHERS = PASSES * (E // GROUP)
 WORD_SPARE = 512
 SCALE_PIECE = SLOTS // 2
-RAW_BUFS = 5
-CODE_BUFS = 4
+RAW_BUFS = 6
+CODE_BUFS = 5
 BANKS = 8
 BANK = 512
-Y_AFTER = 7
+Y_AFTER = 11
+ORDER = [(g, o) for o in range(PASSES) for g in (0, 1)] + [(2, o) for o in range(PASSES)]
 SETS = [(e, min(e + 2, E)) for e in range(0, E, 2)]
 LAST_PIECES = ((0, 2), (2, 4), (4, 5))
 TURNED = 2 * BANK
@@ -49,7 +50,6 @@ def tile_moe_pkd_lin_none_kernel(tc, x_words, x_scales, w, gate, offs, pos1, pos
         scales = held.tile([P, SLOTS], U8, name="scales", align_bytes=64)
         slot_scales = held.tile([P, SLOTS], U8, name="slot_scales", align_bytes=64)
         last_scales = held.tile([P, SLOTS], U8, name="last_scales", align_bytes=64)
-        gate_sb = [held.tile([P, T], F32, name="gate_sb%d" % r) for r in range(TOP)]
         ident = held.tile([P, P], F32, name="ident")
 
         def word_start(o):
@@ -69,6 +69,8 @@ def tile_moe_pkd_lin_none_kernel(tc, x_words, x_scales, w, gate, offs, pos1, pos
             else:
                 raw[e] = ring.tile([P, PASSES, PACK, N], F32, name="raw", tag="raw", bufs=RAW_BUFS)
             nc.sync.dma_start(out=raw[e][:], in_=w[e].rearrange("(o p j) n -> p o j n", p=P, j=PACK))
+            if e % 2 == 1 and e // 2 < PASSES:
+                load_words(e // 2)
 
         scales32 = scales[:].bitcast(I32)
         nc.vector.memset(scales32[:, : T // 4], 0)
@@ -82,9 +84,11 @@ def tile_moe_pkd_lin_none_kernel(tc, x_words, x_scales, w, gate, offs, pos1, pos
         for q in range(4):
             nc.sync.dma_start(out=scales32[32 * q : 32 * q + 16, : T // 4], in_=xs32[0:4, 4 * q : 4 * q + 4, :])
         nc.sync.dma_start(out=scales32[16:32, : T // 4], in_=xs32[4])
-        for o in range(PASSES):
-            load_weights(o)
-            load_words(o)
+        for e in range(RAW_BUFS - 1):
+            load_weights(e)
+        for r, pos in enumerate((pos1, pos2, pos3)):
+            nc.sync.dma_start(pos_sb[r][:], pos)
+        load_weights(RAW_BUFS - 1)
 
         for h in range(SLOTS // SCALE_PIECE):
             cols = SCALE_PIECE // 16
@@ -97,13 +101,12 @@ def tile_moe_pkd_lin_none_kernel(tc, x_words, x_scales, w, gate, offs, pos1, pos
                 out=last_scales[:].bitcast(I32)[32 * q : 32 * q + 4, :],
                 in_=slot_scales[:].bitcast(I32)[16 + 4 * q : 20 + 4 * q, :],
             )
-        for r, pos in enumerate((pos1, pos2, pos3)):
-            nc.sync.dma_start(pos_sb[r][:], pos)
 
         rounded, codes, code_scales, sums, gathered = {}, {}, {}, {}, {}
         passes_gathered = [0] * E
         passes_done = [0] * E
         ys = []
+        gate_sb = []
 
         def cast(s):
             a, b = SETS[s]
@@ -130,7 +133,7 @@ def tile_moe_pkd_lin_none_kernel(tc, x_words, x_scales, w, gate, offs, pos1, pos
                         out=sums[e][:],
                         lhsT=codes[e][:, o * N : (o + 1) * N].bitcast(FP8X4),
                         lhsT_scale=code_scales[e][:, o * N : (o + 1) * N],
-                        rhs=gathered[g * PASSES + o][:, c * C : (c + 1) * C].bitcast(FP8X4),
+                        rhs=gathered[g, o][:, c * C : (c + 1) * C].bitcast(FP8X4),
                         rhs_scale=plane,
                         start=(o == 0),
                         stop=(o == PASSES - 1),
@@ -155,12 +158,12 @@ def tile_moe_pkd_lin_none_kernel(tc, x_words, x_scales, w, gate, offs, pos1, pos
         def gather_words(first, count, tag):
             dest = held.tile([P, count * GROUP_SLOTS], U32, name="dest", tag=tag, align_bytes=64)
             for i in range(first, first + count):
-                g, o = divmod(i, PASSES)
-                gathered[i] = dest[:, (i - first) * GROUP_SLOTS : (i - first + 1) * GROUP_SLOTS]
+                g, o = ORDER[i]
+                gathered[g, o] = dest[:, (i - first) * GROUP_SLOTS : (i - first + 1) * GROUP_SLOTS]
                 window = words[:, word_start(o) : word_start(o) + T + WORD_SPARE].bitcast(U32)
                 for a, b in LAST_PIECES if i == GATHERS - 1 else ((0, GROUP),):
                     cols = slice((g * GROUP + a) * C // 16, (g * GROUP + b) * C // 16)
-                    nc.vector.tensor_copy(gathered[i][:, a * C : b * C], window.indirect(offs_sb[:, cols]))
+                    nc.vector.tensor_copy(gathered[g, o][:, a * C : b * C], window.indirect(offs_sb[:, cols]))
                     for e in range(g * GROUP + a, g * GROUP + b):
                         passes_gathered[e] = o + 1
                     multiply()
@@ -176,10 +179,11 @@ def tile_moe_pkd_lin_none_kernel(tc, x_words, x_scales, w, gate, offs, pos1, pos
         for s in range(len(SETS)):
             if s + 1 < len(SETS):
                 cast(s + 1)
-            if s == 4:
+            if s == 5:
                 for r in range(TOP):
+                    gate_sb.append(ring.tile([P, T], F32, name="gate_sb", tag="raw", bufs=RAW_BUFS))
                     nc.sync.dma_start(out=gate_sb[r][:], in_=gate[r])
-            if s == 3:
+            if s == 4:
                 copy_out(range(0, GROUP))
             if s == 5:
                 copy_out(range(GROUP, 2 * GROUP))

@@ -21,6 +21,7 @@ ADD = mybir.AluOpType.add
 P = 128
 PACK = 4
 PASSES = K // (P * PACK)
+UNIT = N * PACK
 GROUP = 5
 GROUP_SLOTS = GROUP * C
 GATHERS = PASSES * (E // GROUP)
@@ -73,7 +74,7 @@ def tile_moe_pkd_lin_none_kernel(tc, x_words, x_scales, w, gate, offs, pos1, pos
                 load_words(e // 2)
 
         scales32 = scales[:].bitcast(I32)
-        nc.vector.memset(scales32[:, : T // 4], 0)
+        nc.gpsimd.memset(scales32[:, : T // 4], 0)
         nc.vector.memset(scales32[:, T // 4 :], 0)
         nc.vector.memset(words[:, PASSES * T :], 0)
         nc.vector.memset(last_scales[:].bitcast(I32), 0)
@@ -110,12 +111,25 @@ def tile_moe_pkd_lin_none_kernel(tc, x_words, x_scales, w, gate, offs, pos1, pos
 
         def cast(s):
             a, b = SETS[s]
-            rounded[s] = held.tile([P, (b - a) * K], BF16, name="rounded", tag="slot%d" % s, align_bytes=64)
+            cut = (b - a) * (PASSES - 1)
+            rounded[s] = (
+                held.tile([P, cut * UNIT], BF16, name="rounded", tag="slot%d" % s, align_bytes=64),
+                ring.tile([P, (b - a) * UNIT], BF16, name="rounded_rest", tag="rest", bufs=3, align_bytes=64),
+            )
             for e in range(a, b):
-                nc.scalar.copy(
-                    out=rounded[s][:, (e - a) * K : (e - a + 1) * K].rearrange("p (o c i j) -> p o c j i", o=PASSES, i=4, j=PACK),
-                    in_=raw[e][:].rearrange("p o j (c i) -> p o c j i", i=4),
-                )
+                if e + 1 < b:
+                    pieces = ((0, 0, 0, PASSES),)
+                elif b - a == 2:
+                    pieces = ((1, 0, 3, 4), (0, PASSES, 0, 3), (1, 1, 4, 5))
+                else:
+                    pieces = ((1, 0, 4, 5), (0, 0, 0, 4))
+                for part, at, lo, hi in pieces:
+                    nc.scalar.copy(
+                        out=rounded[s][part][:, at * UNIT : (at + hi - lo) * UNIT].rearrange(
+                            "p (o c i j) -> p o c j i", o=hi - lo, i=4, j=PACK
+                        ),
+                        in_=raw[e][:, lo:hi].rearrange("p o j (c i) -> p o c j i", i=4),
+                    )
                 if e + RAW_BUFS < E:
                     load_weights(e + RAW_BUFS)
 
@@ -146,10 +160,8 @@ def tile_moe_pkd_lin_none_kernel(tc, x_words, x_scales, w, gate, offs, pos1, pos
             set_codes = ring.tile([P, width], U32, name="set_codes", tag="codes", bufs=CODE_BUFS, align_bytes=64)
             set_scales = ring.tile([P, width], U8, name="set_scales", tag="code_scales", bufs=CODE_BUFS, align_bytes=64)
             cut = width * 4 // 5
-            for lo, hi in ((0, cut), (cut, width)):
-                nc.vector.quantize_mx(
-                    out=set_codes[:, lo:hi].bitcast(FP8X4), scales=set_scales[:, lo:hi], in_=rounded[s][:, PACK * lo : PACK * hi]
-                )
+            for part, lo, hi in ((0, 0, cut), (1, cut, width)):
+                nc.vector.quantize_mx(out=set_codes[:, lo:hi].bitcast(FP8X4), scales=set_scales[:, lo:hi], in_=rounded[s][part][:])
             for e in range(a, b):
                 codes[e] = set_codes[:, (e - a) * PASSES * N : (e - a + 1) * PASSES * N]
                 code_scales[e] = set_scales[:, (e - a) * PASSES * N : (e - a + 1) * PASSES * N]

from contextlib import ExitStack

import concourse.mybir as mybir
from concourse.masks import make_identity

K, T, E, C, N = 2560, 1280, 15, 256, 128
TOP = 3
SLOTS = E * C
FLOPS = 2 * K * N * SLOTS

F32 = mybir.dt.float32
BF16 = mybir.dt.bfloat16
I32 = mybir.dt.int32
U32 = mybir.dt.uint32
U16 = mybir.dt.uint16
U8 = mybir.dt.uint8
FP8X4 = mybir.dt.float8_e4m3fn_x4
MULT = mybir.AluOpType.mult
ADD = mybir.AluOpType.add

P = 128
PACK = 4
PASSES = K // (P * PACK)
UNIT = N * PACK
GROUP = 5
GROUP_SLOTS = GROUP * C
GATHERS = PASSES * (E // GROUP)
WORD_SPARE = 512
SCALE_PIECE = SLOTS // 2
RAW_BUFS = 6
CODE_BUFS = 5
BANKS = 8
BANK = 512
Y_AFTER = 11
ORDER = [(g, o) for o in range(PASSES) for g in (0, 1)] + [(2, o) for o in range(PASSES)]
SETS = [(e, min(e + 2, E)) for e in range(0, E, 2)]
LAST_PIECES = ((0, 2), (2, 4), (4, 5))
TURNED = 2 * BANK


def tile_moe_pkd_lin_none_kernel(tc, x_words, x_scales, w, gate, offs, pos1, pos2, pos3, out):
    nc = tc.nc
    with ExitStack() as ctx:
        held = ctx.enter_context(tc.tile_pool(name="held", bufs=1))
        ring = ctx.enter_context(tc.tile_pool(name="ring", bufs=1))
        psum = ctx.enter_context(tc.psum_pool(name="psum", bufs=1))

        offs_sb = held.tile([P, SLOTS // 16], U16, name="offs_sb")
        pos_sb = [held.tile([P, T // 16], U16, name="pos_sb%d" % r) for r in range(TOP)]
        words = held.tile([P, PASSES * T + WORD_SPARE], I32, name="words", align_bytes=64)
        scales = held.tile([P, SLOTS], U8, name="scales", align_bytes=64)
        slot_scales = held.tile([P, SLOTS], U8, name="slot_scales", align_bytes=64)
        last_scales = held.tile([P, SLOTS], U8, name="last_scales", align_bytes=64)
        ident = held.tile([P, P], F32, name="ident")

        def word_start(o):
            return (PASSES - 1 - o) * T

        def load_words(o):
            nc.sync.dma_start(
                out=words[:, word_start(o) : word_start(o) + T],
                in_=x_words[o].rearrange("p t r -> p (t r)").bitcast(I32),
            )

        raw = {}

        def load_weights(e):
            if e == Y_AFTER:
                raw[e] = held.tile([P, PASSES, PACK, N], F32, name="raw_y", tag="y")
            else:
                raw[e] = ring.tile([P, PASSES, PACK, N], F32, name="raw", tag="raw", bufs=RAW_BUFS)
            nc.sync.dma_start(out=raw[e][:], in_=w[e].rearrange("(o p j) n -> p o j n", p=P, j=PACK))
            if e % 2 == 1 and e // 2 < PASSES:
                load_words(e // 2)

        scales32 = scales[:].bitcast(I32)
        nc.gpsimd.memset(scales32[:, : T // 4], 0)
        nc.vector.memset(scales32[:, T // 4 :], 0)
        nc.vector.memset(words[:, PASSES * T :], 0)
        nc.vector.memset(last_scales[:].bitcast(I32), 0)
        make_identity(nc, ident[:])

        nc.sync.dma_start(offs_sb[:], offs)
        xs32 = x_scales.bitcast(I32)
        for q in range(4):
            nc.sync.dma_start(out=scales32[32 * q : 32 * q + 16, : T // 4], in_=xs32[0:4, 4 * q : 4 * q + 4, :])
        nc.sync.dma_start(out=scales32[16:32, : T // 4], in_=xs32[4])
        for e in range(RAW_BUFS - 1):
            load_weights(e)
        for r, pos in enumerate((pos1, pos2, pos3)):
            nc.sync.dma_start(pos_sb[r][:], pos)
        load_weights(RAW_BUFS - 1)

        for h in range(SLOTS // SCALE_PIECE):
            cols = SCALE_PIECE // 16
            nc.vector.tensor_copy(
                slot_scales[:, h * SCALE_PIECE : (h + 1) * SCALE_PIECE],
                scales[:].indirect(offs_sb[:, h * cols : (h + 1) * cols]),
            )
        for q in range(4):
            nc.sync.dma_start(
                out=last_scales[:].bitcast(I32)[32 * q : 32 * q + 4, :],
                in_=slot_scales[:].bitcast(I32)[16 + 4 * q : 20 + 4 * q, :],
            )

        rounded, codes, code_scales, sums, gathered = {}, {}, {}, {}, {}
        passes_gathered = [0] * E
        passes_done = [0] * E
        ys = []
        gate_sb = []

        def cast(s):
            a, b = SETS[s]
            cut = (b - a) * (PASSES - 1)
            rounded[s] = (
                held.tile([P, cut * UNIT], BF16, name="rounded", tag="slot%d" % s, align_bytes=64),
                ring.tile([P, (b - a) * UNIT], BF16, name="rounded_rest", tag="rest", bufs=3, align_bytes=64),
            )
            for e in range(a, b):
                if e + 1 < b:
                    pieces = ((0, 0, 0, PASSES),)
                elif b - a == 2:
                    pieces = ((1, 0, 3, 4), (0, PASSES, 0, 3), (1, 1, 4, 5))
                else:
                    pieces = ((1, 0, 4, 5), (0, 0, 0, 4))
                for part, at, lo, hi in pieces:
                    nc.scalar.copy(
                        out=rounded[s][part][:, at * UNIT : (at + hi - lo) * UNIT].rearrange(
                            "p (o c i j) -> p o c j i", o=hi - lo, i=4, j=PACK
                        ),
                        in_=raw[e][:, lo:hi].rearrange("p o j (c i) -> p o c j i", i=4),
                    )
                if e + RAW_BUFS < E:
                    load_weights(e + RAW_BUFS)

        def multiply():
            for e in sorted(codes):
                g, c = divmod(e, GROUP)
                for o in range(passes_done[e], passes_gathered[e]):
                    if o == 0:
                        sums[e] = psum.tile([P, C], F32, name="sums", tag="bank%d" % (e % BANKS))
                    if o < PASSES - 1:
                        plane = slot_scales[4 * o : P, e * C : (e + 1) * C]
                    else:
                        plane = last_scales[:, e * C : (e + 1) * C]
                    nc.tensor.matmul_mx(
                        out=sums[e][:],
                        lhsT=codes[e][:, o * N : (o + 1) * N].bitcast(FP8X4),
                        lhsT_scale=code_scales[e][:, o * N : (o + 1) * N],
                        rhs=gathered[g, o][:, c * C : (c + 1) * C].bitcast(FP8X4),
                        rhs_scale=plane,
                        start=(o == 0),
                        stop=(o == PASSES - 1),
                    )
                passes_done[e] = passes_gathered[e]

        def quantise(s):
            a, b = SETS[s]
            width = (b - a) * PASSES * N
            set_codes = ring.tile([P, width], U32, name="set_codes", tag="codes", bufs=CODE_BUFS, align_bytes=64)
            set_scales = ring.tile([P, width], U8, name="set_scales", tag="code_scales", bufs=CODE_BUFS, align_bytes=64)
            cut = width * 4 // 5
            for part, lo, hi in ((0, 0, cut), (1, cut, width)):
                nc.vector.quantize_mx(out=set_codes[:, lo:hi].bitcast(FP8X4), scales=set_scales[:, lo:hi], in_=rounded[s][part][:])
            for e in range(a, b):
                codes[e] = set_codes[:, (e - a) * PASSES * N : (e - a + 1) * PASSES * N]
                code_scales[e] = set_scales[:, (e - a) * PASSES * N : (e - a + 1) * PASSES * N]
            multiply()

        def gather_words(first, count, tag):
            dest = held.tile([P, count * GROUP_SLOTS], U32, name="dest", tag=tag, align_bytes=64)
            for i in range(first, first + count):
                g, o = ORDER[i]
                gathered[g, o] = dest[:, (i - first) * GROUP_SLOTS : (i - first + 1) * GROUP_SLOTS]
                window = words[:, word_start(o) : word_start(o) + T + WORD_SPARE].bitcast(U32)
                for a, b in LAST_PIECES if i == GATHERS - 1 else ((0, GROUP),):
                    cols = slice((g * GROUP + a) * C // 16, (g * GROUP + b) * C // 16)
                    nc.vector.tensor_copy(gathered[g, o][:, a * C : b * C], window.indirect(offs_sb[:, cols]))
                    for e in range(g * GROUP + a, g * GROUP + b):
                        passes_gathered[e] = o + 1
                    multiply()

        def copy_out(experts):
            if not ys:
                ys.append(held.tile([P, SLOTS], F32, name="y", tag="y"))
            for e in experts:
                nc.scalar.copy(out=ys[0][:, e * C : (e + 1) * C], in_=sums[e][:])

        gather_words(0, 2, "lead")
        cast(0)
        for s in range(len(SETS)):
            if s + 1 < len(SETS):
                cast(s + 1)
            if s == 5:
                for r in range(TOP):
                    gate_sb.append(ring.tile([P, T], F32, name="gate_sb", tag="raw", bufs=RAW_BUFS))
                    nc.sync.dma_start(out=gate_sb[r][:], in_=gate[r])
            if s == 4:
                copy_out(range(0, GROUP))
            if s == 5:
                copy_out(range(GROUP, 2 * GROUP))
            quantise(s)
            if s < 6:
                gather_words(2 * s + 2, 2, "slot%d" % s)
            if s == 7:
                gather_words(GATHERS - 1, 1, "slot%d" % s)
        copy_out(range(2 * GROUP, E))

        y = ys[0]
        prods = [held.tile([P, T], F32, name="prod%d" % r, tag="slot%d" % r, align_bytes=64) for r in range(TOP)]
        turned_sb = held.tile([P, TURNED], F32, name="turned_sb", tag="slot3", align_bytes=64)
        total = held.tile([P, T], F32, name="total", tag="slot4", align_bytes=64)
        part = held.tile([P, T - TURNED], F32, name="part", tag="slot5", align_bytes=64)
        turned = [psum.tile([P, BANK], F32, name="turned%d" % u, tag="bank%d" % u) for u in range(2)]

        def product(r, a, b):
            nc.vector.tensor_tensor(prods[r][:, a:b], y[:].indirect(pos_sb[r][:, a // 16 : b // 16]), gate_sb[r][:, a:b], MULT)

        def add_turned(r, u):
            for k in range(BANK // P):
                nc.tensor.matmul(
                    turned[u][:, k * P : (k + 1) * P],
                    prods[r][:, u * BANK + k * P : u * BANK + (k + 1) * P],
                    ident[:],
                    is_transpose=True,
                    start=(r == 0 and k == 0),
                    stop=(r == TOP - 1 and k == BANK // P - 1),
                )

        def turn_back(u):
            cols = slice(u * BANK, (u + 1) * BANK)
            nc.scalar.copy(out=turned_sb[:, cols], in_=turned[u][:])
            back = psum.tile([P, BANK], F32, name="back", tag="bank%d" % (2 + u))
            for k in range(BANK // P):
                nc.tensor.transpose(back[:, k * P : (k + 1) * P], turned_sb[:, u * BANK + k * P : u * BANK + (k + 1) * P], ident[:])
            nc.scalar.copy(out=total[:, cols], in_=back[:])
            nc.sync.dma_start(out=out[:, cols], in_=total[:, cols])

        for r in range(TOP - 1):
            product(r, 0, TURNED)
            for u in range(2):
                add_turned(r, u)
        for u in range(2):
            product(TOP - 1, u * BANK, (u + 1) * BANK)
            add_turned(TOP - 1, u)
            turn_back(u)
        product(0, TURNED, T)
        product(1, TURNED, T)
        product(2, TURNED, T)
        nc.vector.tensor_tensor(part[:], prods[0][:, TURNED:], prods[1][:, TURNED:], ADD)
        nc.vector.tensor_tensor(total[:, TURNED:], part[:], prods[2][:, TURNED:], ADD)
        nc.sync.dma_start(out=out[:, TURNED:], in_=total[:, TURNED:])
